import numpy as np
import ml_dtypes


def mxq(x, axis, fmt="e4m3"):
    dtype, down = {"e4m3": (ml_dtypes.float8_e4m3fn, 7), "e5m2": (ml_dtypes.float8_e5m2, 14)}[fmt]
    v = np.moveaxis(np.asarray(x, np.float32).astype(ml_dtypes.bfloat16).astype(np.float64), axis, -1)
    blocks = v.reshape(v.shape[:-1] + (-1, 32))
    amax = np.abs(blocks).max(-1, keepdims=True)
    byte = np.maximum(np.where(amax > 0, np.frexp(amax)[1] - 1 + 127, 0) - down, 1)
    scale = np.exp2(byte - 127.0)
    codes = (blocks / scale).astype(np.float32).astype(dtype).astype(np.float64)
    return np.moveaxis((codes * scale).reshape(v.shape), -1, axis)


WIDE = False


def mx_kscale(k):
    if not WIDE:
        return np.ones(k)
    levels = np.array([10, -10, 5, -5, 0])
    if k % 512:
        return np.exp2(np.random.permutation(np.resize(levels, k // 32))).repeat(32)
    a = np.empty((k // 512, 16))
    for p in range(k // 512):
        a[p, :8] = np.random.permutation(np.resize(levels, 8))
        for g in range(8):
            far = levels[np.abs(levels - a[p, g]) >= 10]
            a[p, g + 8] = far[np.random.randint(len(far))]
    return np.exp2(a.ravel()).repeat(32)


def f64(x):
    return np.asarray(x).astype(np.float64)


def striped8(idx):
    return np.asarray(idx).reshape(8, -1, 16).transpose(0, 2, 1).reshape(128, -1).astype(np.uint16)


def unstriped8(offs):
    return offs.reshape(8, 16, -1).transpose(0, 2, 1).reshape(8, -1).astype(np.int64)


def pick8(x, idx, run):
    r = np.arange(len(x))
    return x[r[:, None], idx[r % (8 * run) // run]]


E2M1 = np.array([0.0, 0.5, 1.0, 1.5, 2.0, 3.0, 4.0, 6.0, -0.0, -0.5, -1.0, -1.5, -2.0, -3.0, -4.0, -6.0])


def pack_weight(w, fmt):
    k, n = w.shape
    w = f64(np.asarray(w, np.float32).astype(ml_dtypes.bfloat16)).reshape(k // 32, 32, n)
    amax = np.abs(w).max(1)
    if fmt == "e4m3":
        byte = np.frexp(amax)[1] - 1 + 127 - 7
    else:
        mant, ex = np.frexp(amax / 6.0)
        byte = np.where(mant > 0.5, ex, ex - 1) + 127
    byte = np.clip(np.where(amax > 0, byte, 1), 1, 254)
    scaled = (w * np.exp2(127.0 - byte)[:, None, :]).reshape(k, n).astype(np.float32)
    by_word = np.ascontiguousarray(scaled.reshape(k // 512, 128, 4, n).transpose(0, 1, 3, 2))
    if fmt == "e4m3":
        words = by_word.astype(ml_dtypes.float8_e4m3fn).view(np.uint8)
    else:
        c = by_word.astype(ml_dtypes.float4_e2m1fn).view(np.uint8) & 0xF
        words = (c[..., 0::2] | (c[..., 1::2] << 4)).reshape(k // 512, 128, 2 * n)
    return np.ascontiguousarray(words), np.ascontiguousarray(byte.astype(np.uint8).reshape(k // 512, 16, n))


def unpack_weight(words, scales, fmt):
    g, _, n = scales.shape
    words = np.ascontiguousarray(words).reshape(g, 128, n, -1)
    if fmt == "e4m3":
        vals = words.view(ml_dtypes.float8_e4m3fn).astype(np.float64)
    else:
        nib = np.empty((g, 128, n, 4), np.uint8)
        nib[..., 0::2] = words & 0xF
        nib[..., 1::2] = words >> 4
        vals = E2M1[nib]
    vals = vals * np.repeat(np.exp2(scales.astype(np.float64) - 127.0), 8, axis=1)[..., None]
    return vals.transpose(0, 1, 3, 2).reshape(g * 512, n)


D, T, U, X, I, O, Q = 512, 1024, 1024, 1024, 512, 2048, 128


def setup_inputs():
    n = np.random.standard_normal
    idx = np.stack([np.random.permutation(X)[:I] for _ in range(8)])
    idx2 = np.stack([np.random.permutation(O)[:I] for _ in range(8)])
    idx3 = np.stack([np.random.permutation(O)[:I] for _ in range(8)])
    idx4 = np.stack([np.random.permutation(X)[:I] for _ in range(8)])
    idx5 = np.stack([np.random.permutation(X)[:I] for _ in range(8)])
    fd = mx_kscale(D)
    cachep = pack_weight(n((D, T)) / fd[:, None], "e2m1")
    draftp = pack_weight(n((D, U)) / fd[:, None], "e4m3")
    archp = pack_weight(n((D, X)) / fd[:, None], "e2m1")
    return {
        "query": (n((D, Q)) * 1.0 / np.sqrt(D) * fd[:, None]).astype(np.float32),
        "cache_words": cachep[0],
        "cache_scales": cachep[1],
        "draft_words": draftp[0],
        "draft_scales": draftp[1],
        "arch_words": archp[0],
        "arch_scales": archp[1],
        "offs": striped8(idx),
        "offs2": striped8(idx2),
        "offs3": striped8(idx3),
        "offs4": striped8(idx4),
        "offs5": striped8(idx5),
    }


def reference(query, cache_words, cache_scales, draft_words, draft_scales, arch_words, arch_scales, offs, offs2, offs3, offs4, offs5):
    idx = unstriped8(offs)
    idx2 = unstriped8(offs2)
    idx3 = unstriped8(offs3)
    idx4 = unstriped8(offs4)
    idx5 = unstriped8(offs5)
    cacheu = unpack_weight(cache_words, cache_scales, "e2m1")
    draftu = unpack_weight(draft_words, draft_scales, "e4m3")
    archu = unpack_weight(arch_words, arch_scales, "e2m1")
    queryq = mxq(f64(query), 0, "e4m3")
    a = queryq.T @ cacheu
    b = queryq.T @ draftu
    c0 = queryq.T @ archu
    ab = np.concatenate([a, b], axis=1)
    f1 = np.zeros((Q, O))
    f1[np.arange(Q)[:, None], idx2[np.arange(Q) % 128 // 16]] = pick8(c0, idx, 16)
    r = ab - f1
    f2 = np.zeros((Q, X))
    f2[np.arange(Q)[:, None], idx4[np.arange(Q) % 128 // 16]] = pick8(r, idx3, 16)
    cc = c0 + f2
    y = np.maximum(pick8(cc, idx5, 16), pick8(r, idx3, 16))
    return y

@@ -1,0 +1,161 @@
+from contextlib import ExitStack
+
+import concourse.mybir as mybir
+
+D, T, U, X, I, O, Q = 512, 1024, 1024, 1024, 512, 2048, 128
+FLOPS = 2 * D * Q * (T + U + X)
+
+F32 = mybir.dt.float32
+BF16 = mybir.dt.bfloat16
+I32 = mybir.dt.int32
+U32 = mybir.dt.uint32
+U16 = mybir.dt.uint16
+U8 = mybir.dt.uint8
+FP8X4 = mybir.dt.float8_e4m3fn_x4
+FP4X4 = mybir.dt.float4_e2m1fn_x4
+COPY = mybir.ActivationFunctionType.Copy
+ALU = mybir.AluOpType
+
+P = 128
+PACK = 4
+BANK = 512
+HALF = I // 2
+ARCH_N = 256
+R_POOL = 576
+CC_POOL = 256
+Q_VEC = 80
+
+
+def load_plane(nc, plane, scales):
+    for quad in range(4):
+        nc.sync.dma_start(
+            out=plane[32 * quad : 32 * quad + 4, :].bitcast(I32),
+            in_=scales[0, 4 * quad : 4 * quad + 4, :].bitcast(I32),
+        )
+
+
+def tile_attend_jointthree_three_kernel(
+    tc, query, cache_words, cache_scales, draft_words, draft_scales, arch_words, arch_scales,
+    offs, offs2, offs3, offs4, offs5, out,
+):
+    nc = tc.nc
+    with ExitStack() as ctx:
+        lists = ctx.enter_context(tc.tile_pool(name="lists", bufs=1))
+        sb = ctx.enter_context(tc.tile_pool(name="sb", bufs=1))
+        ps = ctx.enter_context(tc.psum_pool(name="ps", bufs=1))
+
+        arch_plane = sb.tile([P, X], U8, align_bytes=64)
+        cache_plane = sb.tile([P, T], U8, align_bytes=64)
+        draft_plane = sb.tile([P, U], U8, align_bytes=64)
+        f1 = sb.tile([P, O], F32, align_bytes=64)
+        for plane in (arch_plane, cache_plane, draft_plane):
+            nc.vector.memset(plane[:].bitcast(U32), 0)
+        nc.vector.memset(f1[:], 0.0)
+
+        q_raw = sb.tile([P, PACK, Q], F32, align_bytes=64, tag="cache_then_f2")
+        nc.sync.dma_start(out=q_raw[:], in_=query.rearrange("(p j) q -> p j q", j=PACK))
+        arch_w = sb.tile([P, 2 * X], U8, align_bytes=64)
+        nc.sync.dma_start(out=arch_w[:].bitcast(I32), in_=arch_words[0].bitcast(I32))
+        load_plane(nc, arch_plane, arch_scales)
+        idx = lists.tile([P, I // 16], U16)
+        nc.sync.dma_start(idx[:], offs)
+        idx2 = lists.tile([P, I // 16], U16)
+        nc.sync.dma_start(idx2[:], offs2)
+
+        q_bf = sb.tile([P, Q, PACK], BF16, align_bytes=64, tag="qbf_then_draft")
+        q_by_column = q_raw[:].rearrange("p j q -> p q j")
+        nc.vector.tensor_copy(out=q_bf[:, 0:Q_VEC, :], in_=q_by_column[:, 0:Q_VEC, :])
+        nc.scalar.copy(out=q_bf[:, Q_VEC:Q, :], in_=q_by_column[:, Q_VEC:Q, :])
+        q_codes = sb.tile([P, Q], U32, align_bytes=64)
+        q_plane = sb.tile([P, Q], U8, align_bytes=64)
+        nc.vector.quantize_mx(
+            out=q_codes[:].bitcast(FP8X4), scales=q_plane[:], in_=q_bf[:].rearrange("p q j -> p (q j)")
+        )
+
+        cache_w = sb.tile([P, 2 * T], U8, align_bytes=64, tag="cache_then_f2")
+        nc.sync.dma_start(out=cache_w[:].bitcast(I32), in_=cache_words[0].bitcast(I32))
+        load_plane(nc, cache_plane, cache_scales)
+        draft_w = sb.tile([P, U], U32, align_bytes=64, tag="qbf_then_draft")
+        nc.sync.dma_start(
+            out=draft_w[:].bitcast(I32),
+            in_=draft_words[0].rearrange("p n t -> p (n t)").bitcast(I32),
+        )
+        load_plane(nc, draft_plane, draft_scales)
+        idx3 = lists.tile([P, I // 16], U16)
+        nc.sync.dma_start(idx3[:], offs3)
+        idx4 = lists.tile([P, I // 16], U16)
+        nc.sync.dma_start(idx4[:], offs4)
+        idx5 = lists.tile([P, I // 16], U16)
+        nc.sync.dma_start(idx5[:], offs5)
+
+        def score(bank, words, plane):
+            nc.tensor.matmul_mx(
+                out=bank, lhsT=q_codes[:].bitcast(FP8X4), lhsT_scale=q_plane[:],
+                rhs=words, rhs_scale=plane, start=True, stop=True,
+            )
+
+        c0 = sb.tile([P, X], F32, align_bytes=64)
+        c0_banks = []
+        for n in range(X // ARCH_N):
+            lo, hi = n * ARCH_N, (n + 1) * ARCH_N
+            bank = ps.tile([P, ARCH_N], F32, name="c0_bank%d" % n)
+            score(bank[:], arch_w[:, 2 * lo : 2 * hi].bitcast(FP4X4), arch_plane[:, lo:hi])
+            if n % 2 == 0:
+                nc.vector.tensor_copy(out=c0[:, lo:hi], in_=bank[:])
+            else:
+                nc.scalar.activation(c0[:, lo:hi], bank[:], COPY)
+            c0_banks.append(bank)
+
+        ab_banks = []
+        for n in range(T // BANK):
+            lo, hi = n * BANK, (n + 1) * BANK
+            bank = ps.tile([P, BANK], F32, name="a_bank%d" % n)
+            score(bank[:], cache_w[:, 2 * lo : 2 * hi].bitcast(FP4X4), cache_plane[:, lo:hi])
+            ab_banks.append(bank)
+        for n in range(U // BANK):
+            lo, hi = n * BANK, (n + 1) * BANK
+            bank = ps.tile([P, BANK], F32, name="b_bank%d" % n)
+            score(bank[:], draft_w[:, lo:hi].bitcast(FP8X4), draft_plane[:, lo:hi])
+            ab_banks.append(bank)
+
+        halves = [(slice(h * HALF, (h + 1) * HALF), slice(h * HALF // 16, (h + 1) * HALF // 16)) for h in range(2)]
+        for h, (slots, cols) in enumerate(halves):
+            picked_c0 = sb.tile([P, HALF], F32, align_bytes=64, name="picked_c0_%d" % h)
+            nc.vector.tensor_copy(picked_c0[:], c0[:].indirect(idx[:, cols]))
+            nc.scalar.activation(f1[:].indirect(idx2[:, cols]), picked_c0[:], COPY)
+
+        f2 = sb.tile([P, X], F32, align_bytes=64, tag="cache_then_f2")
+        nc.gpsimd.memset(f2[:], 0.0)
+
+        r = sb.tile([P, O], F32, align_bytes=64)
+        ab_head = sb.tile([P, R_POOL], F32, align_bytes=64)
+        for n, bank in enumerate(ab_banks):
+            lo, hi = n * BANK, min((n + 1) * BANK, R_POOL)
+            if lo < hi:
+                nc.vector.tensor_copy(out=ab_head[:, lo:hi], in_=bank[:, 0 : hi - lo])
+        nc.gpsimd.tensor_tensor(r[:, 0:R_POOL], ab_head[:], f1[:, 0:R_POOL], ALU.subtract)
+        for n, bank in enumerate(ab_banks):
+            lo, hi = max(n * BANK, R_POOL), (n + 1) * BANK
+            if lo < hi:
+                nc.vector.tensor_tensor(r[:, lo:hi], bank[:, lo - n * BANK : BANK], f1[:, lo:hi], ALU.subtract)
+
+        picked_r = sb.tile([P, I], F32, align_bytes=64)
+        nc.vector.tensor_copy(picked_r[:], r[:].indirect(idx3[:]))
+        nc.scalar.activation(f2[:].indirect(idx4[:]), picked_r[:], COPY)
+
+        cc = sb.tile([P, X], F32, align_bytes=64)
+        nc.gpsimd.tensor_tensor(cc[:, 0:CC_POOL], c0[:, 0:CC_POOL], f2[:, 0:CC_POOL], ALU.add)
+        for n, bank in enumerate(c0_banks):
+            lo, hi = max(n * ARCH_N, CC_POOL), (n + 1) * ARCH_N
+            if lo < hi:
+                nc.vector.tensor_tensor(cc[:, lo:hi], bank[:, lo - n * ARCH_N : ARCH_N], f2[:, lo:hi], ALU.add)
+
+        for h, (slots, cols) in enumerate(halves):
+            picked_cc = sb.tile([P, HALF], F32, align_bytes=64, name="picked_cc_%d" % h)
+            if h == 0:
+                nc.vector.tensor_copy(picked_cc[:], cc[:].indirect(idx5[:, cols]))
+            else:
+                nc.scalar.activation(picked_cc[:], cc[:].indirect(idx5[:, cols]), COPY)
+            y = sb.tile([P, HALF], F32, align_bytes=64, name="y_%d" % h)
+            nc.vector.tensor_tensor(y[:], picked_cc[:], picked_r[:, slots], ALU.max)
+            nc.sync.dma_start(out=out[:, slots], in_=y[:])

@@ -20,9 +20,10 @@ P = 128
 PACK = 4
 BANK = 512
 HALF = I // 2
-ARCH_N = 256
-R_POOL = 576
-CC_POOL = 256
+ARCH_CUTS = (0, 512, 768, 896, 1024)
+F1_VEC = 1536
+R_POOL = 608
+CC_VEC = 736
 Q_VEC = 80
 
 
@@ -48,9 +49,11 @@ def tile_attend_jointthree_three_kernel(
         cache_plane = sb.tile([P, T], U8, align_bytes=64)
         draft_plane = sb.tile([P, U], U8, align_bytes=64)
         f1 = sb.tile([P, O], F32, align_bytes=64)
-        for plane in (arch_plane, cache_plane, draft_plane):
-            nc.vector.memset(plane[:].bitcast(U32), 0)
-        nc.vector.memset(f1[:], 0.0)
+        nc.vector.memset(arch_plane[:].bitcast(U32), 0)
+        nc.vector.memset(f1[:, 0:F1_VEC], 0.0)
+        nc.gpsimd.memset(cache_plane[:].bitcast(U32), 0)
+        nc.gpsimd.memset(draft_plane[:].bitcast(U32), 0)
+        nc.gpsimd.memset(f1[:, F1_VEC:O], 0.0)
 
         q_raw = sb.tile([P, PACK, Q], F32, align_bytes=64, tag="cache_then_f2")
         nc.sync.dma_start(out=q_raw[:], in_=query.rearrange("(p j) q -> p j q", j=PACK))
@@ -96,9 +99,9 @@ def tile_attend_jointthree_three_kernel(
 
         c0 = sb.tile([P, X], F32, align_bytes=64)
         c0_banks = []
-        for n in range(X // ARCH_N):
-            lo, hi = n * ARCH_N, (n + 1) * ARCH_N
-            bank = ps.tile([P, ARCH_N], F32, name="c0_bank%d" % n)
+        for n in range(len(ARCH_CUTS) - 1):
+            lo, hi = ARCH_CUTS[n], ARCH_CUTS[n + 1]
+            bank = ps.tile([P, hi - lo], F32, name="c0_bank%d" % n)
             score(bank[:], arch_w[:, 2 * lo : 2 * hi].bitcast(FP4X4), arch_plane[:, lo:hi])
             if n % 2 == 0:
                 nc.vector.tensor_copy(out=c0[:, lo:hi], in_=bank[:])
@@ -119,10 +122,10 @@ def tile_attend_jointthree_three_kernel(
             ab_banks.append(bank)
 
         halves = [(slice(h * HALF, (h + 1) * HALF), slice(h * HALF // 16, (h + 1) * HALF // 16)) for h in range(2)]
-        for h, (slots, cols) in enumerate(halves):
-            picked_c0 = sb.tile([P, HALF], F32, align_bytes=64, name="picked_c0_%d" % h)
-            nc.vector.tensor_copy(picked_c0[:], c0[:].indirect(idx[:, cols]))
-            nc.scalar.activation(f1[:].indirect(idx2[:, cols]), picked_c0[:], COPY)
+        picked_c0 = sb.tile([P, I], F32, align_bytes=64)
+        nc.vector.tensor_copy(picked_c0[:, halves[0][0]], c0[:].indirect(idx[:, halves[0][1]]))
+        nc.scalar.activation(picked_c0[:, halves[1][0]], c0[:].indirect(idx[:, halves[1][1]]), COPY)
+        nc.scalar.activation(f1[:].indirect(idx2[:]), picked_c0[:], COPY)
 
         f2 = sb.tile([P, X], F32, align_bytes=64, tag="cache_then_f2")
         nc.gpsimd.memset(f2[:], 0.0)
@@ -144,11 +147,11 @@ def tile_attend_jointthree_three_kernel(
         nc.scalar.activation(f2[:].indirect(idx4[:]), picked_r[:], COPY)
 
         cc = sb.tile([P, X], F32, align_bytes=64)
-        nc.gpsimd.tensor_tensor(cc[:, 0:CC_POOL], c0[:, 0:CC_POOL], f2[:, 0:CC_POOL], ALU.add)
+        nc.gpsimd.tensor_tensor(cc[:, CC_VEC:X], c0[:, CC_VEC:X], f2[:, CC_VEC:X], ALU.add)
         for n, bank in enumerate(c0_banks):
-            lo, hi = max(n * ARCH_N, CC_POOL), (n + 1) * ARCH_N
+            lo, hi = ARCH_CUTS[n], min(ARCH_CUTS[n + 1], CC_VEC)
             if lo < hi:
-                nc.vector.tensor_tensor(cc[:, lo:hi], bank[:, lo - n * ARCH_N : ARCH_N], f2[:, lo:hi], ALU.add)
+                nc.vector.tensor_tensor(cc[:, lo:hi], bank[:, 0 : hi - lo], f2[:, lo:hi], ALU.add)
 
         for h, (slots, cols) in enumerate(halves):
             picked_cc = sb.tile([P, HALF], F32, align_bytes=64, name="picked_cc_%d" % h)

@@ -55,7 +55,7 @@ def tile_attend_jointthree_three_kernel(
         nc.gpsimd.memset(draft_plane[:].bitcast(U32), 0)
         nc.gpsimd.memset(f1[:, F1_VEC:O], 0.0)
 
-        q_raw = sb.tile([P, PACK, Q], F32, align_bytes=64, tag="cache_then_f2")
+        q_raw = sb.tile([P, PACK, Q], F32, align_bytes=64)
         nc.sync.dma_start(out=q_raw[:], in_=query.rearrange("(p j) q -> p j q", j=PACK))
         arch_w = sb.tile([P, 2 * X], U8, align_bytes=64)
         nc.sync.dma_start(out=arch_w[:].bitcast(I32), in_=arch_words[0].bitcast(I32))
@@ -65,7 +65,7 @@ def tile_attend_jointthree_three_kernel(
         idx2 = lists.tile([P, I // 16], U16)
         nc.sync.dma_start(idx2[:], offs2)
 
-        q_bf = sb.tile([P, Q, PACK], BF16, align_bytes=64, tag="qbf_then_draft")
+        q_bf = sb.tile([P, Q, PACK], BF16, align_bytes=64)
         q_by_column = q_raw[:].rearrange("p j q -> p q j")
         nc.vector.tensor_copy(out=q_bf[:, 0:Q_VEC, :], in_=q_by_column[:, 0:Q_VEC, :])
         nc.scalar.copy(out=q_bf[:, Q_VEC:Q, :], in_=q_by_column[:, Q_VEC:Q, :])
@@ -78,7 +78,7 @@ def tile_attend_jointthree_three_kernel(
         cache_w = sb.tile([P, 2 * T], U8, align_bytes=64, tag="cache_then_f2")
         nc.sync.dma_start(out=cache_w[:].bitcast(I32), in_=cache_words[0].bitcast(I32))
         load_plane(nc, cache_plane, cache_scales)
-        draft_w = sb.tile([P, U], U32, align_bytes=64, tag="qbf_then_draft")
+        draft_w = sb.tile([P, U], U32, align_bytes=64)
         nc.sync.dma_start(
             out=draft_w[:].bitcast(I32),
             in_=draft_words[0].rearrange("p n t -> p (n t)").bitcast(I32),

@@ -21,9 +21,8 @@ PACK = 4
 BANK = 512
 HALF = I // 2
 ARCH_CUTS = (0, 512, 768, 896, 1024)
-F1_VEC = 1536
-R_POOL = 608
-CC_VEC = 736
+R_POOL = 672
+CC_VEC = 688
 Q_VEC = 80
 
 
@@ -49,11 +48,9 @@ def tile_attend_jointthree_three_kernel(
         cache_plane = sb.tile([P, T], U8, align_bytes=64)
         draft_plane = sb.tile([P, U], U8, align_bytes=64)
         f1 = sb.tile([P, O], F32, align_bytes=64)
-        nc.vector.memset(arch_plane[:].bitcast(U32), 0)
-        nc.vector.memset(f1[:, 0:F1_VEC], 0.0)
-        nc.gpsimd.memset(cache_plane[:].bitcast(U32), 0)
-        nc.gpsimd.memset(draft_plane[:].bitcast(U32), 0)
-        nc.gpsimd.memset(f1[:, F1_VEC:O], 0.0)
+        for plane in (arch_plane, cache_plane, draft_plane):
+            nc.vector.memset(plane[:].bitcast(U32), 0)
+        nc.vector.memset(f1[:], 0.0)
 
         q_raw = sb.tile([P, PACK, Q], F32, align_bytes=64)
         nc.sync.dma_start(out=q_raw[:], in_=query.rearrange("(p j) q -> p j q", j=PACK))

from contextlib import ExitStack

import concourse.mybir as mybir

D, T, U, X, I, O, Q = 512, 1024, 1024, 1024, 512, 2048, 128
FLOPS = 2 * D * Q * (T + U + X)

F32 = mybir.dt.float32
BF16 = mybir.dt.bfloat16
I32 = mybir.dt.int32
U32 = mybir.dt.uint32
U16 = mybir.dt.uint16
U8 = mybir.dt.uint8
FP8X4 = mybir.dt.float8_e4m3fn_x4
FP4X4 = mybir.dt.float4_e2m1fn_x4
COPY = mybir.ActivationFunctionType.Copy
ALU = mybir.AluOpType

P = 128
PACK = 4
BANK = 512
HALF = I // 2
ARCH_CUTS = (0, 512, 768, 896, 1024)
R_POOL = 672
CC_VEC = 688
Q_VEC = 80


def load_plane(nc, plane, scales):
    for quad in range(4):
        nc.sync.dma_start(
            out=plane[32 * quad : 32 * quad + 4, :].bitcast(I32),
            in_=scales[0, 4 * quad : 4 * quad + 4, :].bitcast(I32),
        )


def tile_attend_jointthree_three_kernel(
    tc, query, cache_words, cache_scales, draft_words, draft_scales, arch_words, arch_scales,
    offs, offs2, offs3, offs4, offs5, out,
):
    nc = tc.nc
    with ExitStack() as ctx:
        lists = ctx.enter_context(tc.tile_pool(name="lists", bufs=1))
        sb = ctx.enter_context(tc.tile_pool(name="sb", bufs=1))
        ps = ctx.enter_context(tc.psum_pool(name="ps", bufs=1))

        arch_plane = sb.tile([P, X], U8, align_bytes=64)
        cache_plane = sb.tile([P, T], U8, align_bytes=64)
        draft_plane = sb.tile([P, U], U8, align_bytes=64)
        f1 = sb.tile([P, O], F32, align_bytes=64)
        for plane in (arch_plane, cache_plane, draft_plane):
            nc.vector.memset(plane[:].bitcast(U32), 0)
        nc.vector.memset(f1[:], 0.0)

        q_raw = sb.tile([P, PACK, Q], F32, align_bytes=64)
        nc.sync.dma_start(out=q_raw[:], in_=query.rearrange("(p j) q -> p j q", j=PACK))
        arch_w = sb.tile([P, 2 * X], U8, align_bytes=64)
        nc.sync.dma_start(out=arch_w[:].bitcast(I32), in_=arch_words[0].bitcast(I32))
        load_plane(nc, arch_plane, arch_scales)
        idx = lists.tile([P, I // 16], U16)
        nc.sync.dma_start(idx[:], offs)
        idx2 = lists.tile([P, I // 16], U16)
        nc.sync.dma_start(idx2[:], offs2)

        q_bf = sb.tile([P, Q, PACK], BF16, align_bytes=64)
        q_by_column = q_raw[:].rearrange("p j q -> p q j")
        nc.vector.tensor_copy(out=q_bf[:, 0:Q_VEC, :], in_=q_by_column[:, 0:Q_VEC, :])
        nc.scalar.copy(out=q_bf[:, Q_VEC:Q, :], in_=q_by_column[:, Q_VEC:Q, :])
        q_codes = sb.tile([P, Q], U32, align_bytes=64)
        q_plane = sb.tile([P, Q], U8, align_bytes=64)
        nc.vector.quantize_mx(
            out=q_codes[:].bitcast(FP8X4), scales=q_plane[:], in_=q_bf[:].rearrange("p q j -> p (q j)")
        )

        cache_w = sb.tile([P, 2 * T], U8, align_bytes=64, tag="cache_then_f2")
        nc.sync.dma_start(out=cache_w[:].bitcast(I32), in_=cache_words[0].bitcast(I32))
        load_plane(nc, cache_plane, cache_scales)
        draft_w = sb.tile([P, U], U32, align_bytes=64)
        nc.sync.dma_start(
            out=draft_w[:].bitcast(I32),
            in_=draft_words[0].rearrange("p n t -> p (n t)").bitcast(I32),
        )
        load_plane(nc, draft_plane, draft_scales)
        idx3 = lists.tile([P, I // 16], U16)
        nc.sync.dma_start(idx3[:], offs3)
        idx4 = lists.tile([P, I // 16], U16)
        nc.sync.dma_start(idx4[:], offs4)
        idx5 = lists.tile([P, I // 16], U16)
        nc.sync.dma_start(idx5[:], offs5)

        def score(bank, words, plane):
            nc.tensor.matmul_mx(
                out=bank, lhsT=q_codes[:].bitcast(FP8X4), lhsT_scale=q_plane[:],
                rhs=words, rhs_scale=plane, start=True, stop=True,
            )

        c0 = sb.tile([P, X], F32, align_bytes=64)
        c0_banks = []
        for n in range(len(ARCH_CUTS) - 1):
            lo, hi = ARCH_CUTS[n], ARCH_CUTS[n + 1]
            bank = ps.tile([P, hi - lo], F32, name="c0_bank%d" % n)
            score(bank[:], arch_w[:, 2 * lo : 2 * hi].bitcast(FP4X4), arch_plane[:, lo:hi])
            if n % 2 == 0:
                nc.vector.tensor_copy(out=c0[:, lo:hi], in_=bank[:])
            else:
                nc.scalar.activation(c0[:, lo:hi], bank[:], COPY)
            c0_banks.append(bank)

        ab_banks = []
        for n in range(T // BANK):
            lo, hi = n * BANK, (n + 1) * BANK
            bank = ps.tile([P, BANK], F32, name="a_bank%d" % n)
            score(bank[:], cache_w[:, 2 * lo : 2 * hi].bitcast(FP4X4), cache_plane[:, lo:hi])
            ab_banks.append(bank)
        for n in range(U // BANK):
            lo, hi = n * BANK, (n + 1) * BANK
            bank = ps.tile([P, BANK], F32, name="b_bank%d" % n)
            score(bank[:], draft_w[:, lo:hi].bitcast(FP8X4), draft_plane[:, lo:hi])
            ab_banks.append(bank)

        halves = [(slice(h * HALF, (h + 1) * HALF), slice(h * HALF // 16, (h + 1) * HALF // 16)) for h in range(2)]
        picked_c0 = sb.tile([P, I], F32, align_bytes=64)
        nc.vector.tensor_copy(picked_c0[:, halves[0][0]], c0[:].indirect(idx[:, halves[0][1]]))
        nc.scalar.activation(picked_c0[:, halves[1][0]], c0[:].indirect(idx[:, halves[1][1]]), COPY)
        nc.scalar.activation(f1[:].indirect(idx2[:]), picked_c0[:], COPY)

        f2 = sb.tile([P, X], F32, align_bytes=64, tag="cache_then_f2")
        nc.gpsimd.memset(f2[:], 0.0)

        r = sb.tile([P, O], F32, align_bytes=64)
        ab_head = sb.tile([P, R_POOL], F32, align_bytes=64)
        for n, bank in enumerate(ab_banks):
            lo, hi = n * BANK, min((n + 1) * BANK, R_POOL)
            if lo < hi:
                nc.vector.tensor_copy(out=ab_head[:, lo:hi], in_=bank[:, 0 : hi - lo])
        nc.gpsimd.tensor_tensor(r[:, 0:R_POOL], ab_head[:], f1[:, 0:R_POOL], ALU.subtract)
        for n, bank in enumerate(ab_banks):
            lo, hi = max(n * BANK, R_POOL), (n + 1) * BANK
            if lo < hi:
                nc.vector.tensor_tensor(r[:, lo:hi], bank[:, lo - n * BANK : BANK], f1[:, lo:hi], ALU.subtract)

        picked_r = sb.tile([P, I], F32, align_bytes=64)
        nc.vector.tensor_copy(picked_r[:], r[:].indirect(idx3[:]))
        nc.scalar.activation(f2[:].indirect(idx4[:]), picked_r[:], COPY)

        cc = sb.tile([P, X], F32, align_bytes=64)
        nc.gpsimd.tensor_tensor(cc[:, CC_VEC:X], c0[:, CC_VEC:X], f2[:, CC_VEC:X], ALU.add)
        for n, bank in enumerate(c0_banks):
            lo, hi = ARCH_CUTS[n], min(ARCH_CUTS[n + 1], CC_VEC)
            if lo < hi:
                nc.vector.tensor_tensor(cc[:, lo:hi], bank[:, 0 : hi - lo], f2[:, lo:hi], ALU.add)

        for h, (slots, cols) in enumerate(halves):
            picked_cc = sb.tile([P, HALF], F32, align_bytes=64, name="picked_cc_%d" % h)
            if h == 0:
                nc.vector.tensor_copy(picked_cc[:], cc[:].indirect(idx5[:, cols]))
            else:
                nc.scalar.activation(picked_cc[:], cc[:].indirect(idx5[:, cols]), COPY)
            y = sb.tile([P, HALF], F32, align_bytes=64, name="y_%d" % h)
            nc.vector.tensor_tensor(y[:], picked_cc[:], picked_r[:, slots], ALU.max)
            nc.sync.dma_start(out=out[:, slots], in_=y[:])
